import numpy as np
import ml_dtypes


def mxq(x, axis, fmt="e4m3"):
    dtype, down = {"e4m3": (ml_dtypes.float8_e4m3fn, 7), "e5m2": (ml_dtypes.float8_e5m2, 14)}[fmt]
    v = np.moveaxis(np.asarray(x, np.float32).astype(ml_dtypes.bfloat16).astype(np.float64), axis, -1)
    blocks = v.reshape(v.shape[:-1] + (-1, 32))
    amax = np.abs(blocks).max(-1, keepdims=True)
    byte = np.maximum(np.where(amax > 0, np.frexp(amax)[1] - 1 + 127, 0) - down, 1)
    scale = np.exp2(byte - 127.0)
    codes = (blocks / scale).astype(np.float32).astype(dtype).astype(np.float64)
    return np.moveaxis((codes * scale).reshape(v.shape), -1, axis)


WIDE = False


def mx_kscale(k):
    if not WIDE:
        return np.ones(k)
    levels = np.array([10, -10, 5, -5, 0])
    if k % 512:
        return np.exp2(np.random.permutation(np.resize(levels, k // 32))).repeat(32)
    a = np.empty((k // 512, 16))
    for p in range(k // 512):
        a[p, :8] = np.random.permutation(np.resize(levels, 8))
        for g in range(8):
            far = levels[np.abs(levels - a[p, g]) >= 10]
            a[p, g + 8] = far[np.random.randint(len(far))]
    return np.exp2(a.ravel()).repeat(32)


def f64(x):
    return np.asarray(x).astype(np.float64)


def striped8(idx):
    return np.asarray(idx).reshape(8, -1, 16).transpose(0, 2, 1).reshape(128, -1).astype(np.uint16)


def unstriped8(offs):
    return offs.reshape(8, 16, -1).transpose(0, 2, 1).reshape(8, -1).astype(np.int64)


def pick8(x, idx, run):
    r = np.arange(len(x))
    return x[r[:, None], idx[r % (8 * run) // run]]


E2M1 = np.array([0.0, 0.5, 1.0, 1.5, 2.0, 3.0, 4.0, 6.0, -0.0, -0.5, -1.0, -1.5, -2.0, -3.0, -4.0, -6.0])


def pack_weight(w, fmt):
    k, n = w.shape
    w = f64(np.asarray(w, np.float32).astype(ml_dtypes.bfloat16)).reshape(k // 32, 32, n)
    amax = np.abs(w).max(1)
    if fmt == "e4m3":
        byte = np.frexp(amax)[1] - 1 + 127 - 7
    else:
        mant, ex = np.frexp(amax / 6.0)
        byte = np.where(mant > 0.5, ex, ex - 1) + 127
    byte = np.clip(np.where(amax > 0, byte, 1), 1, 254)
    scaled = (w * np.exp2(127.0 - byte)[:, None, :]).reshape(k, n).astype(np.float32)
    by_word = np.ascontiguousarray(scaled.reshape(k // 512, 128, 4, n).transpose(0, 1, 3, 2))
    if fmt == "e4m3":
        words = by_word.astype(ml_dtypes.float8_e4m3fn).view(np.uint8)
    else:
        c = by_word.astype(ml_dtypes.float4_e2m1fn).view(np.uint8) & 0xF
        words = (c[..., 0::2] | (c[..., 1::2] << 4)).reshape(k // 512, 128, 2 * n)
    return np.ascontiguousarray(words), np.ascontiguousarray(byte.astype(np.uint8).reshape(k // 512, 16, n))


def unpack_weight(words, scales, fmt):
    g, _, n = scales.shape
    words = np.ascontiguousarray(words).reshape(g, 128, n, -1)
    if fmt == "e4m3":
        vals = words.view(ml_dtypes.float8_e4m3fn).astype(np.float64)
    else:
        nib = np.empty((g, 128, n, 4), np.uint8)
        nib[..., 0::2] = words & 0xF
        nib[..., 1::2] = words >> 4
        vals = E2M1[nib]
    vals = vals * np.repeat(np.exp2(scales.astype(np.float64) - 127.0), 8, axis=1)[..., None]
    return vals.transpose(0, 1, 3, 2).reshape(g * 512, n)


D, V, Q, I, G = 512, 2048, 128, 512, 64


def setup_inputs():
    n = np.random.standard_normal
    idx = np.stack([np.random.permutation(V)[:I] for _ in range(8)])
    fd = mx_kscale(D)
    vocp = pack_weight(n((D, V)) / fd[:, None], "e2m1")
    return {
        "hid": (n((D, Q)) * 1.0 / np.sqrt(D) * fd[:, None]).astype(np.float32),
        "voc_words": vocp[0],
        "voc_scales": vocp[1],
        "target": (np.random.uniform(0.0, 0.1, (Q, G))).astype(np.float32),
        "dhid": (n((D, Q)) * 1.0 / np.sqrt(D) * fd[:, None]).astype(np.float32),
        "base": (0.5 * n((Q, V))).astype(np.float32),
        "offs": striped8(idx),
    }


def reference(hid, voc_words, voc_scales, target, dhid, base, offs):
    idx = unstriped8(offs)
    vocu = unpack_weight(voc_words, voc_scales, "e2m1")
    hidq = mxq(f64(hid), 0, "e4m3")
    a = hidq.T @ vocu
    dhidq = mxq(f64(dhid), 0, "e4m3")
    ta = dhidq.T @ vocu
    m1 = np.max(a, axis=1, keepdims=True)
    p = np.exp(a - m1)
    z = np.sum(p, axis=1, keepdims=True)
    px = np.exp(pick8(a, idx, 16) - m1)
    u1 = px.reshape(Q, G, I // G).sum(axis=2) / z
    du1 = f64(target) / u1
    e1 = du1 / z
    r1 = np.repeat(e1, I // G, axis=1)
    dz = np.sum(du1 * px.reshape(Q, G, I // G).sum(axis=2) / np.square(z) * (-1.0), axis=1, keepdims=True)
    xp = ta * p
    xz = np.sum(xp, axis=1, keepdims=True)
    xpx = pick8(ta, idx, 16) * px
    xu1 = (xpx.reshape(Q, G, I // G).sum(axis=2) - xz * px.reshape(Q, G, I // G).sum(axis=2) / z) / z
    xdu1 = xu1 * f64(target) / np.square(u1) * (-1.0)
    xe1 = (xdu1 - xz * du1 / z) / z
    xr1 = np.repeat(xe1, I // G, axis=1)
    xdz = np.sum((xdu1 * px.reshape(Q, G, I // G).sum(axis=2) + xpx.reshape(Q, G, I // G).sum(axis=2) * du1 - xz * z * 2.0 * du1 * px.reshape(Q, G, I // G).sum(axis=2) / np.square(z)) / np.square(z) * (-1.0), axis=1, keepdims=True)
    xe2 = xr1 * px + xpx * r1
    xs2 = np.zeros((Q, V))
    xs2[np.arange(Q)[:, None], idx[np.arange(Q) % 128 // 16]] = xe2
    xda = xdz * p + xp * dz + xs2
    y = xda * 64.0 + f64(base)
    return y

@@ -1,0 +1,222 @@
+from contextlib import ExitStack
+
+import concourse.mybir as mybir
+from concourse.masks import make_identity
+
+D, V, Q, I, G = 512, 2048, 128, 512, 64
+FLOPS = 2 * 2 * D * Q * V
+
+F32 = mybir.dt.float32
+BF16 = mybir.dt.bfloat16
+I32 = mybir.dt.int32
+U32 = mybir.dt.uint32
+U16 = mybir.dt.uint16
+U8 = mybir.dt.uint8
+FP8X4 = mybir.dt.float8_e4m3fn_x4
+FP4X4 = mybir.dt.float4_e2m1fn_x4
+ALU = mybir.AluOpType
+ACT = mybir.ActivationFunctionType
+AX = mybir.AxisListType
+
+P = 128
+PACK = 4
+BANK = 512
+NB = V // BANK
+GROUP = I // G
+NU = 1
+
+
+def tile_attend_hvgroupshare_heads_kernel(tc, hid, voc_words, voc_scales, target, dhid, base, offs, out):
+    nc = tc.nc
+    with ExitStack() as ctx:
+        sb = ctx.enter_context(tc.tile_pool(name="sb", bufs=1))
+        ps = ctx.enter_context(tc.psum_pool(name="ps", bufs=1))
+
+        def cols(b):
+            return slice(b * BANK, (b + 1) * BANK)
+
+        voc_sc = sb.tile([P, V], U8, name="voc_sc", align_bytes=64)
+        nc.vector.memset(voc_sc[:].bitcast(I32), 0)
+        hid_raw = sb.tile([P, PACK, Q], F32, name="hid_raw")
+        nc.sync.dma_start(out=hid_raw[:], in_=hid.rearrange("(p j) q -> p j q", j=PACK))
+        words = [sb.tile([P, V], U8, name="words%d" % h, align_bytes=64) for h in range(2)]
+        nc.sync.dma_start(out=words[0][:].bitcast(I32), in_=voc_words[0, :, 0:V].bitcast(I32))
+        for quad in range(4):
+            nc.sync.dma_start(
+                out=voc_sc[32 * quad : 32 * quad + 4, :].bitcast(I32),
+                in_=voc_scales[0, 4 * quad : 4 * quad + 4, :].bitcast(I32),
+            )
+        nc.sync.dma_start(out=words[1][:].bitcast(I32), in_=voc_words[0, :, V : 2 * V].bitcast(I32))
+        dhid_raw = sb.tile([P, PACK, Q], F32, name="dhid_raw")
+        nc.sync.dma_start(out=dhid_raw[:], in_=dhid.rearrange("(p j) q -> p j q", j=PACK))
+        offsets = sb.tile([P, I // 16], U16, name="offsets")
+        nc.sync.dma_start(offsets[:], offs)
+        tgt = sb.tile([P, G], F32, name="tgt")
+        nc.sync.dma_start(out=tgt[:], in_=target)
+        base_sb = [sb.tile([P, V // 2], F32, name="base%d" % h) for h in range(2)]
+        for h in range(2):
+            nc.sync.dma_start(out=base_sb[h][:], in_=base[:, h * (V // 2) : (h + 1) * (V // 2)])
+
+        warm = sb.tile([P, 1], F32, name="warm")
+        nc.gpsimd.memset(warm[:], 0.0)
+        warm_out = sb.tile([P, 1], F32, name="warm_out")
+        nc.scalar.activation(warm_out[:], warm[:], ACT.Exp)
+        ident = sb.tile([P, P], F32, name="ident")
+        make_identity(nc, ident[:])
+        cf = sb.tile([P, NB], F32, name="cf")
+        nc.gpsimd.memset(cf[:], 1.0)
+        xs2 = sb.tile([P, V], F32, name="xs2")
+        nc.gpsimd.memset(xs2[:], 0.0)
+
+        hid_bf = sb.tile([P, Q, PACK], BF16, name="hid_bf", align_bytes=64)
+        nc.vector.tensor_copy(out=hid_bf[:], in_=hid_raw[:].rearrange("p j q -> p q j"))
+        hid_codes = sb.tile([P, Q], U32, name="hid_codes", align_bytes=64)
+        hid_sc = sb.tile([P, Q], U8, name="hid_sc", align_bytes=64)
+        nc.vector.quantize_mx(out=hid_codes[:].bitcast(FP8X4), scales=hid_sc[:], in_=hid_bf[:].rearrange("p q j -> p (q j)"))
+        dhid_bf = sb.tile([P, Q, PACK], BF16, name="dhid_bf", align_bytes=64)
+        nc.scalar.copy(out=dhid_bf[:], in_=dhid_raw[:].rearrange("p j q -> p q j"))
+        dhid_codes = sb.tile([P, Q], U32, name="dhid_codes", align_bytes=64)
+        dhid_sc = sb.tile([P, Q], U8, name="dhid_sc", align_bytes=64)
+        nc.vector.quantize_mx(out=dhid_codes[:].bitcast(FP8X4), scales=dhid_sc[:], in_=dhid_bf[:].rearrange("p q j -> p (q j)"))
+
+        def score(bank, codes, scales, b):
+            half, part = divmod(b, 2)
+            nc.tensor.matmul_mx(
+                out=bank[:],
+                lhsT=codes[:].bitcast(FP8X4),
+                lhsT_scale=scales[:],
+                rhs=words[half][:, part * 2 * BANK : (part + 1) * 2 * BANK].bitcast(FP4X4),
+                rhs_scale=voc_sc[:, cols(b)],
+                start=True,
+                stop=True,
+            )
+
+        a_ps = [ps.tile([P, BANK], F32, name="a_ps%d" % b, tag="x%d" % b) for b in range(NB)]
+        ta_ps = [ps.tile([P, BANK], F32, name="ta_ps%d" % b, tag="y%d" % b) for b in range(NB)]
+        for b in range(NB):
+            score(a_ps[b], hid_codes, hid_sc, b)
+        for b in range(NB):
+            score(ta_ps[b], dhid_codes, dhid_sc, b)
+
+        a_sb = sb.tile([P, V], F32, name="a_sb")
+        ta_sb = sb.tile([P, V], F32, name="ta_sb")
+        p_sb = sb.tile([P, V], F32, name="p_sb")
+        bmax = sb.tile([P, NB], F32, name="bmax")
+        nrun = sb.tile([P, NB], F32, name="nrun")
+        zb = sb.tile([P, NB], F32, name="zb")
+        fb = sb.tile([P, NB], F32, name="fb")
+        for b in range(NB):
+            nc.vector.tensor_scalar(a_sb[:, cols(b)], a_ps[b][:], 1.0, None, ALU.mult, ALU.max, accum_out=bmax[:, b : b + 1])
+            if b == 0:
+                nc.gpsimd.tensor_scalar(nrun[:, 0:1], bmax[:, 0:1], -1.0, 0.0, ALU.mult, ALU.add)
+            else:
+                nc.gpsimd.tensor_scalar(nrun[:, b : b + 1], bmax[:, b : b + 1], -1.0, nrun[:, b - 1 : b], ALU.mult, ALU.min)
+            if b == NB - 1:
+                nc.scalar.activation(fb[:], nrun[:], ACT.Exp, bias=nrun[:, b : b + 1], scale=-1.0)
+            nc.scalar.activation(p_sb[:, cols(b)], a_sb[:, cols(b)], ACT.Exp, bias=nrun[:, b : b + 1], accum_out=zb[:, b : b + 1])
+        neg_m = nrun[:, NB - 1 : NB]
+
+        px = sb.tile([P, I], F32, name="px")
+        ga = sb.tile([P, I], F32, name="ga")
+        nc.vector.tensor_copy(ga[:], a_sb[:].indirect(offsets[:]))
+        nc.scalar.activation(px[:], ga[:], ACT.Exp, bias=neg_m)
+
+        sumT = [ps.tile([P, BANK], F32, name="sumT%d" % b, tag="x%d" % b) for b in range(NB)]
+
+        def add_turned(b, src, first, last):
+            for j in range(BANK // P):
+                nc.tensor.matmul(
+                    sumT[b][:, j * P : (j + 1) * P],
+                    lhsT=src[:, j * P : (j + 1) * P],
+                    rhs=ident[:],
+                    is_transpose=True,
+                    start=first and j == 0,
+                    stop=last and j == BANK // P - 1,
+                )
+
+        for b in range(NB):
+            half, part = divmod(b, 2)
+            add_turned(b, base_sb[half][:, cols(part)], True, False)
+
+        nt = sb.tile([P, 1], F32, name="nt")
+        t64 = sb.tile([P, G], F32, name="t64")
+        nc.scalar.activation(t64[:], tgt[:], ACT.Copy, scale=64.0, accum_out=nt[:])
+        xp = sb.tile([P, V], F32, name="xp")
+        xps = sb.tile([P, NU * BANK], F32, name="xps")
+        acc = sb.tile([P, NB], F32, name="acc")
+        z = sb.tile([P, 1], F32, name="z")
+        zf = sb.tile([P, NB], F32, name="zf")
+        rz = sb.tile([P, 1], F32, name="rz")
+        alpha = sb.tile([P, NB], F32, name="alpha")
+        nfr = sb.tile([P, NB], F32, name="nfr")
+
+        def product(b, scale):
+            nc.vector.scalar_tensor_tensor(xp[:, cols(b)], ta_ps[b][:], scale, p_sb[:, cols(b)], ALU.mult, ALU.mult, accum_out=acc[:, b : b + 1])
+            nc.scalar.copy(ta_sb[:, cols(b)], ta_ps[b][:])
+
+        def grouped(t):
+            return t[:].rearrange("p (g i) -> p g i", i=GROUP)
+
+        def spread(t):
+            return t[:].unsqueeze(2).to_broadcast([P, G, GROUP])
+
+        for b in range(NU):
+            product(b, 1.0)
+        nc.vector.scalar_tensor_tensor(zf[:], zb[:], -1.0, fb[:], ALU.mult, ALU.mult, accum_out=z[:])
+        ssum = sb.tile([P, G], F32, name="ssum")
+        nc.vector.tensor_reduce(ssum[:], grouped(px), AX.X, ALU.add)
+        nc.vector.reciprocal(rz[:], z[:])
+        rs = sb.tile([P, G], F32, name="rs")
+        nc.vector.reciprocal(rs[:], ssum[:])
+        nc.gpsimd.tensor_scalar(alpha[:], fb[:], rz[:], nt[:], ALU.mult, ALU.mult)
+        nc.gpsimd.tensor_scalar(cf[:, 0:NU], fb[:, 0:NU], rz[:], nt[:], ALU.mult, ALU.mult)
+        nc.gpsimd.tensor_scalar(nfr[:], fb[:], rz[:], 0.0, ALU.mult, ALU.add)
+        for b in range(NU):
+            nc.gpsimd.tensor_scalar(xps[:, cols(b)], xp[:, cols(b)], alpha[:, b : b + 1], 0.0, ALU.mult, ALU.add)
+            add_turned(b, xps[:, cols(b)], False, False)
+        ne64 = sb.tile([P, G], F32, name="ne64")
+        nw = sb.tile([P, I], F32, name="nw")
+        nc.gpsimd.tensor_tensor(ne64[:], t64[:], rs[:], ALU.mult)
+        nc.gpsimd.tensor_tensor(grouped(nw), grouped(px), spread(ne64), ALU.mult)
+        for b in range(NU, NB):
+            product(b, alpha[:, b : b + 1])
+            add_turned(b, xp[:, cols(b)], False, False)
+        kk = sb.tile([P, 1], F32, name="kk")
+        accf = sb.tile([P, NB], F32, name="accf")
+        nc.vector.scalar_tensor_tensor(accf[:], acc[:], 1.0, cf[:], ALU.mult, ALU.mult, accum_out=kk[:])
+        beta = sb.tile([P, NB], F32, name="beta")
+        nc.gpsimd.tensor_scalar(beta[:], nfr[:], kk[:], 0.0, ALU.mult, ALU.add)
+
+        y = sb.tile([P, I], F32, name="y")
+        nc.vector.tensor_tensor(y[:], ta_sb[:].indirect(offsets[:]), nw[:], ALU.mult)
+        ysum = sb.tile([P, G], F32, name="ysum")
+        nc.vector.tensor_reduce(ysum[:], grouped(y), AX.X, ALU.add)
+        nf = sb.tile([P, G], F32, name="nf")
+        nc.vector.scalar_tensor_tensor(nf[:], ysum[:], -1.0, rs[:], ALU.mult, ALU.mult)
+        v = sb.tile([P, I], F32, name="v")
+        nc.vector.tensor_tensor(grouped(v), grouped(px), spread(nf), ALU.mult)
+        nc.vector.tensor_tensor(xs2[:].indirect(offsets[:]), y[:], v[:], ALU.add)
+
+        u1 = sb.tile([P, V], F32, name="u1")
+        turned = sb.tile([P, V], F32, name="turned")
+        dense = [ps.tile([P, BANK], F32, name="dense%d" % b, tag="y%d" % b) for b in range(NB)]
+
+        def scale_p(b):
+            nc.scalar.activation(u1[:, cols(b)], p_sb[:, cols(b)], ACT.Copy, scale=beta[:, b : b + 1])
+            add_turned(b, u1[:, cols(b)], False, True)
+
+        def turn_back(b):
+            nc.scalar.copy(turned[:, cols(b)], sumT[b][:])
+            for j in range(BANK // P):
+                nc.tensor.transpose(dense[b][:, j * P : (j + 1) * P], turned[:, b * BANK + j * P : b * BANK + (j + 1) * P], ident[:])
+
+        scale_p(0)
+        for b in range(1, NB):
+            scale_p(b)
+            turn_back(b - 1)
+        turn_back(NB - 1)
+
+        res = sb.tile([P, V], F32, name="res")
+        for b in range(NB):
+            nc.vector.tensor_tensor(res[:, cols(b)], dense[b][:], xs2[:, cols(b)], ALU.add)
+            nc.sync.dma_start(out=out[:, cols(b)], in_=res[:, cols(b)])

@@ -36,17 +36,16 @@ def tile_attend_hvgroupshare_heads_kernel(tc, hid, voc_words, voc_scales, target
             return slice(b * BANK, (b + 1) * BANK)
 
         voc_sc = sb.tile([P, V], U8, name="voc_sc", align_bytes=64)
-        nc.vector.memset(voc_sc[:].bitcast(I32), 0)
         hid_raw = sb.tile([P, PACK, Q], F32, name="hid_raw")
         nc.sync.dma_start(out=hid_raw[:], in_=hid.rearrange("(p j) q -> p j q", j=PACK))
-        words = [sb.tile([P, V], U8, name="words%d" % h, align_bytes=64) for h in range(2)]
-        nc.sync.dma_start(out=words[0][:].bitcast(I32), in_=voc_words[0, :, 0:V].bitcast(I32))
+        words = [sb.tile([P, n * 2 * BANK], U8, name="words%d" % n, align_bytes=64) for n in (1, NB - 1)]
         for quad in range(4):
             nc.sync.dma_start(
                 out=voc_sc[32 * quad : 32 * quad + 4, :].bitcast(I32),
                 in_=voc_scales[0, 4 * quad : 4 * quad + 4, :].bitcast(I32),
             )
-        nc.sync.dma_start(out=words[1][:].bitcast(I32), in_=voc_words[0, :, V : 2 * V].bitcast(I32))
+        nc.sync.dma_start(out=words[0][:].bitcast(I32), in_=voc_words[0, :, 0 : 2 * BANK].bitcast(I32))
+        nc.sync.dma_start(out=words[1][:].bitcast(I32), in_=voc_words[0, :, 2 * BANK : 2 * V].bitcast(I32))
         dhid_raw = sb.tile([P, PACK, Q], F32, name="dhid_raw")
         nc.sync.dma_start(out=dhid_raw[:], in_=dhid.rearrange("(p j) q -> p j q", j=PACK))
         offsets = sb.tile([P, I // 16], U16, name="offsets")
@@ -62,14 +61,14 @@ def tile_attend_hvgroupshare_heads_kernel(tc, hid, voc_words, voc_scales, target
         warm_out = sb.tile([P, 1], F32, name="warm_out")
         nc.scalar.activation(warm_out[:], warm[:], ACT.Exp)
         ident = sb.tile([P, P], F32, name="ident")
-        make_identity(nc, ident[:])
-        cf = sb.tile([P, NB], F32, name="cf")
-        nc.gpsimd.memset(cf[:], 1.0)
+        nc.vector.memset(ident[:], 0.0)
+        make_identity(nc, ident[:], nomemset=True)
         xs2 = sb.tile([P, V], F32, name="xs2")
-        nc.gpsimd.memset(xs2[:], 0.0)
+        nc.vector.memset(xs2[:], 0.0)
 
         hid_bf = sb.tile([P, Q, PACK], BF16, name="hid_bf", align_bytes=64)
-        nc.vector.tensor_copy(out=hid_bf[:], in_=hid_raw[:].rearrange("p j q -> p q j"))
+        nc.vector.tensor_copy(out=hid_bf[:, 0 : Q // 2, :], in_=hid_raw[:, :, 0 : Q // 2].rearrange("p j q -> p q j"))
+        nc.scalar.copy(out=hid_bf[:, Q // 2 : Q, :], in_=hid_raw[:, :, Q // 2 : Q].rearrange("p j q -> p q j"))
         hid_codes = sb.tile([P, Q], U32, name="hid_codes", align_bytes=64)
         hid_sc = sb.tile([P, Q], U8, name="hid_sc", align_bytes=64)
         nc.vector.quantize_mx(out=hid_codes[:].bitcast(FP8X4), scales=hid_sc[:], in_=hid_bf[:].rearrange("p q j -> p (q j)"))
@@ -80,7 +79,7 @@ def tile_attend_hvgroupshare_heads_kernel(tc, hid, voc_words, voc_scales, target
         nc.vector.quantize_mx(out=dhid_codes[:].bitcast(FP8X4), scales=dhid_sc[:], in_=dhid_bf[:].rearrange("p q j -> p (q j)"))
 
         def score(bank, codes, scales, b):
-            half, part = divmod(b, 2)
+            half, part = (0, 0) if b == 0 else (1, b - 1)
             nc.tensor.matmul_mx(
                 out=bank[:],
                 lhsT=codes[:].bitcast(FP8X4),
@@ -110,8 +109,10 @@ def tile_attend_hvgroupshare_heads_kernel(tc, hid, voc_words, voc_scales, target
             if b == 0:
                 nc.gpsimd.tensor_scalar(nrun[:, 0:1], bmax[:, 0:1], -1.0, 0.0, ALU.mult, ALU.add)
             else:
-                nc.gpsimd.tensor_scalar(nrun[:, b : b + 1], bmax[:, b : b + 1], -1.0, nrun[:, b - 1 : b], ALU.mult, ALU.min)
+                eng = nc.vector if b == NB - 1 else nc.gpsimd
+                eng.tensor_scalar(nrun[:, b : b + 1], bmax[:, b : b + 1], -1.0, nrun[:, b - 1 : b], ALU.mult, ALU.min)
             if b == NB - 1:
+                nc.scalar.copy(ta_sb[:, cols(0)], ta_ps[0][:])
                 nc.scalar.activation(fb[:], nrun[:], ACT.Exp, bias=nrun[:, b : b + 1], scale=-1.0)
             nc.scalar.activation(p_sb[:, cols(b)], a_sb[:, cols(b)], ACT.Exp, bias=nrun[:, b : b + 1], accum_out=zb[:, b : b + 1])
         neg_m = nrun[:, NB - 1 : NB]
@@ -120,6 +121,8 @@ def tile_attend_hvgroupshare_heads_kernel(tc, hid, voc_words, voc_scales, target
         ga = sb.tile([P, I], F32, name="ga")
         nc.vector.tensor_copy(ga[:], a_sb[:].indirect(offsets[:]))
         nc.scalar.activation(px[:], ga[:], ACT.Exp, bias=neg_m)
+        for b in range(1, NB):
+            nc.scalar.copy(ta_sb[:, cols(b)], ta_ps[b][:])
 
         sumT = [ps.tile([P, BANK], F32, name="sumT%d" % b, tag="x%d" % b) for b in range(NB)]
 
@@ -144,6 +147,7 @@ def tile_attend_hvgroupshare_heads_kernel(tc, hid, voc_words, voc_scales, target
         xp = sb.tile([P, V], F32, name="xp")
         xps = sb.tile([P, NU * BANK], F32, name="xps")
         acc = sb.tile([P, NB], F32, name="acc")
+        acc0 = sb.tile([P, 1], F32, name="acc0")
         z = sb.tile([P, 1], F32, name="z")
         zf = sb.tile([P, NB], F32, name="zf")
         rz = sb.tile([P, 1], F32, name="rz")
@@ -151,8 +155,7 @@ def tile_attend_hvgroupshare_heads_kernel(tc, hid, voc_words, voc_scales, target
         nfr = sb.tile([P, NB], F32, name="nfr")
 
         def product(b, scale):
-            nc.vector.scalar_tensor_tensor(xp[:, cols(b)], ta_ps[b][:], scale, p_sb[:, cols(b)], ALU.mult, ALU.mult, accum_out=acc[:, b : b + 1])
-            nc.scalar.copy(ta_sb[:, cols(b)], ta_ps[b][:])
+            nc.vector.scalar_tensor_tensor(xp[:, cols(b)], ta_ps[b][:], scale, p_sb[:, cols(b)], ALU.mult, ALU.mult, accum_out=(acc0[:] if b == 0 else acc[:, b : b + 1]))
 
         def grouped(t):
             return t[:].rearrange("p (g i) -> p g i", i=GROUP)
@@ -169,32 +172,37 @@ def tile_attend_hvgroupshare_heads_kernel(tc, hid, voc_words, voc_scales, target
         rs = sb.tile([P, G], F32, name="rs")
         nc.vector.reciprocal(rs[:], ssum[:])
         nc.gpsimd.tensor_scalar(alpha[:], fb[:], rz[:], nt[:], ALU.mult, ALU.mult)
-        nc.gpsimd.tensor_scalar(cf[:, 0:NU], fb[:, 0:NU], rz[:], nt[:], ALU.mult, ALU.mult)
         nc.gpsimd.tensor_scalar(nfr[:], fb[:], rz[:], 0.0, ALU.mult, ALU.add)
         for b in range(NU):
             nc.gpsimd.tensor_scalar(xps[:, cols(b)], xp[:, cols(b)], alpha[:, b : b + 1], 0.0, ALU.mult, ALU.add)
             add_turned(b, xps[:, cols(b)], False, False)
+        nc.scalar.activation(acc[:, 0:1], acc0[:], ACT.Copy, scale=alpha[:, 0:1])
         ne64 = sb.tile([P, G], F32, name="ne64")
         nw = sb.tile([P, I], F32, name="nw")
-        nc.gpsimd.tensor_tensor(ne64[:], t64[:], rs[:], ALU.mult)
-        nc.gpsimd.tensor_tensor(grouped(nw), grouped(px), spread(ne64), ALU.mult)
+        nc.vector.tensor_tensor(ne64[:], t64[:], rs[:], ALU.mult)
+        nc.vector.tensor_tensor(grouped(nw), grouped(px), spread(ne64), ALU.mult)
         for b in range(NU, NB):
             product(b, alpha[:, b : b + 1])
             add_turned(b, xp[:, cols(b)], False, False)
         kk = sb.tile([P, 1], F32, name="kk")
         accf = sb.tile([P, NB], F32, name="accf")
-        nc.vector.scalar_tensor_tensor(accf[:], acc[:], 1.0, cf[:], ALU.mult, ALU.mult, accum_out=kk[:])
+        nc.scalar.activation(accf[:], acc[:], ACT.Copy, accum_out=kk[:])
         beta = sb.tile([P, NB], F32, name="beta")
-        nc.gpsimd.tensor_scalar(beta[:], nfr[:], kk[:], 0.0, ALU.mult, ALU.add)
+        nc.scalar.activation(beta[:], nfr[:], ACT.Copy, scale=kk[:])
 
         y = sb.tile([P, I], F32, name="y")
-        nc.vector.tensor_tensor(y[:], ta_sb[:].indirect(offsets[:]), nw[:], ALU.mult)
         ysum = sb.tile([P, G], F32, name="ysum")
-        nc.vector.tensor_reduce(ysum[:], grouped(y), AX.X, ALU.add)
         nf = sb.tile([P, G], F32, name="nf")
-        nc.vector.scalar_tensor_tensor(nf[:], ysum[:], -1.0, rs[:], ALU.mult, ALU.mult)
         v = sb.tile([P, I], F32, name="v")
-        nc.vector.tensor_tensor(grouped(v), grouped(px), spread(nf), ALU.mult)
+        halves = [(slice(h * I // 2, (h + 1) * I // 2), slice(h * G // 2, (h + 1) * G // 2), slice(h * 16, (h + 1) * 16)) for h in range(2)]
+        for ent, grp, off in halves:
+            nc.vector.tensor_tensor(y[:, ent], ta_sb[:].indirect(offsets[:, off]), nw[:, ent], ALU.mult)
+        for ent, grp, off in halves:
+            nc.vector.tensor_reduce(ysum[:, grp], grouped(y)[:, grp, :], AX.X, ALU.add)
+        for ent, grp, off in halves:
+            nc.vector.scalar_tensor_tensor(nf[:, grp], ysum[:, grp], -1.0, rs[:, grp], ALU.mult, ALU.mult)
+        for ent, grp, off in halves:
+            nc.vector.tensor_tensor(grouped(v)[:, grp, :], grouped(px)[:, grp, :], nf[:, grp].unsqueeze(2).to_broadcast([P, G // 2, GROUP]), ALU.mult)
         nc.vector.tensor_tensor(xs2[:].indirect(offsets[:]), y[:], v[:], ALU.add)
 
         u1 = sb.tile([P, V], F32, name="u1")
@@ -217,6 +225,7 @@ def tile_attend_hvgroupshare_heads_kernel(tc, hid, voc_words, voc_scales, target
         turn_back(NB - 1)
 
         res = sb.tile([P, V], F32, name="res")
-        for b in range(NB):
-            nc.vector.tensor_tensor(res[:, cols(b)], dense[b][:], xs2[:, cols(b)], ALU.add)
-            nc.sync.dma_start(out=out[:, cols(b)], in_=res[:, cols(b)])
+        for lo, hi in ((0, 512), (512, 1024), (1024, 1536), (1536, 2048)):
+            b = lo // BANK
+            nc.vector.tensor_tensor(res[:, lo:hi], dense[b][:, lo - b * BANK : hi - b * BANK], xs2[:, lo:hi], ALU.add)
+            nc.sync.dma_start(out=out[:, lo:hi], in_=res[:, lo:hi])

from contextlib import ExitStack

import concourse.mybir as mybir
from concourse.masks import make_identity

D, V, Q, I, G = 512, 2048, 128, 512, 64
FLOPS = 2 * 2 * D * Q * V

F32 = mybir.dt.float32
BF16 = mybir.dt.bfloat16
I32 = mybir.dt.int32
U32 = mybir.dt.uint32
U16 = mybir.dt.uint16
U8 = mybir.dt.uint8
FP8X4 = mybir.dt.float8_e4m3fn_x4
FP4X4 = mybir.dt.float4_e2m1fn_x4
ALU = mybir.AluOpType
ACT = mybir.ActivationFunctionType
AX = mybir.AxisListType

P = 128
PACK = 4
BANK = 512
NB = V // BANK
GROUP = I // G
NU = 1


def tile_attend_hvgroupshare_heads_kernel(tc, hid, voc_words, voc_scales, target, dhid, base, offs, out):
    nc = tc.nc
    with ExitStack() as ctx:
        sb = ctx.enter_context(tc.tile_pool(name="sb", bufs=1))
        ps = ctx.enter_context(tc.psum_pool(name="ps", bufs=1))

        def cols(b):
            return slice(b * BANK, (b + 1) * BANK)

        voc_sc = sb.tile([P, V], U8, name="voc_sc", align_bytes=64)
        hid_raw = sb.tile([P, PACK, Q], F32, name="hid_raw")
        nc.sync.dma_start(out=hid_raw[:], in_=hid.rearrange("(p j) q -> p j q", j=PACK))
        words = [sb.tile([P, n * 2 * BANK], U8, name="words%d" % n, align_bytes=64) for n in (1, NB - 1)]
        for quad in range(4):
            nc.sync.dma_start(
                out=voc_sc[32 * quad : 32 * quad + 4, :].bitcast(I32),
                in_=voc_scales[0, 4 * quad : 4 * quad + 4, :].bitcast(I32),
            )
        nc.sync.dma_start(out=words[0][:].bitcast(I32), in_=voc_words[0, :, 0 : 2 * BANK].bitcast(I32))
        nc.sync.dma_start(out=words[1][:].bitcast(I32), in_=voc_words[0, :, 2 * BANK : 2 * V].bitcast(I32))
        dhid_raw = sb.tile([P, PACK, Q], F32, name="dhid_raw")
        nc.sync.dma_start(out=dhid_raw[:], in_=dhid.rearrange("(p j) q -> p j q", j=PACK))
        offsets = sb.tile([P, I // 16], U16, name="offsets")
        nc.sync.dma_start(offsets[:], offs)
        tgt = sb.tile([P, G], F32, name="tgt")
        nc.sync.dma_start(out=tgt[:], in_=target)
        base_sb = [sb.tile([P, V // 2], F32, name="base%d" % h) for h in range(2)]
        for h in range(2):
            nc.sync.dma_start(out=base_sb[h][:], in_=base[:, h * (V // 2) : (h + 1) * (V // 2)])

        warm = sb.tile([P, 1], F32, name="warm")
        nc.gpsimd.memset(warm[:], 0.0)
        warm_out = sb.tile([P, 1], F32, name="warm_out")
        nc.scalar.activation(warm_out[:], warm[:], ACT.Exp)
        ident = sb.tile([P, P], F32, name="ident")
        nc.vector.memset(ident[:], 0.0)
        make_identity(nc, ident[:], nomemset=True)
        xs2 = sb.tile([P, V], F32, name="xs2")
        nc.vector.memset(xs2[:], 0.0)

        hid_bf = sb.tile([P, Q, PACK], BF16, name="hid_bf", align_bytes=64)
        nc.vector.tensor_copy(out=hid_bf[:, 0 : Q // 2, :], in_=hid_raw[:, :, 0 : Q // 2].rearrange("p j q -> p q j"))
        nc.scalar.copy(out=hid_bf[:, Q // 2 : Q, :], in_=hid_raw[:, :, Q // 2 : Q].rearrange("p j q -> p q j"))
        hid_codes = sb.tile([P, Q], U32, name="hid_codes", align_bytes=64)
        hid_sc = sb.tile([P, Q], U8, name="hid_sc", align_bytes=64)
        nc.vector.quantize_mx(out=hid_codes[:].bitcast(FP8X4), scales=hid_sc[:], in_=hid_bf[:].rearrange("p q j -> p (q j)"))
        dhid_bf = sb.tile([P, Q, PACK], BF16, name="dhid_bf", align_bytes=64)
        nc.scalar.copy(out=dhid_bf[:], in_=dhid_raw[:].rearrange("p j q -> p q j"))
        dhid_codes = sb.tile([P, Q], U32, name="dhid_codes", align_bytes=64)
        dhid_sc = sb.tile([P, Q], U8, name="dhid_sc", align_bytes=64)
        nc.vector.quantize_mx(out=dhid_codes[:].bitcast(FP8X4), scales=dhid_sc[:], in_=dhid_bf[:].rearrange("p q j -> p (q j)"))

        def score(bank, codes, scales, b):
            half, part = (0, 0) if b == 0 else (1, b - 1)
            nc.tensor.matmul_mx(
                out=bank[:],
                lhsT=codes[:].bitcast(FP8X4),
                lhsT_scale=scales[:],
                rhs=words[half][:, part * 2 * BANK : (part + 1) * 2 * BANK].bitcast(FP4X4),
                rhs_scale=voc_sc[:, cols(b)],
                start=True,
                stop=True,
            )

        a_ps = [ps.tile([P, BANK], F32, name="a_ps%d" % b, tag="x%d" % b) for b in range(NB)]
        ta_ps = [ps.tile([P, BANK], F32, name="ta_ps%d" % b, tag="y%d" % b) for b in range(NB)]
        for b in range(NB):
            score(a_ps[b], hid_codes, hid_sc, b)
        for b in range(NB):
            score(ta_ps[b], dhid_codes, dhid_sc, b)

        a_sb = sb.tile([P, V], F32, name="a_sb")
        ta_sb = sb.tile([P, V], F32, name="ta_sb")
        p_sb = sb.tile([P, V], F32, name="p_sb")
        bmax = sb.tile([P, NB], F32, name="bmax")
        nrun = sb.tile([P, NB], F32, name="nrun")
        zb = sb.tile([P, NB], F32, name="zb")
        fb = sb.tile([P, NB], F32, name="fb")
        for b in range(NB):
            nc.vector.tensor_scalar(a_sb[:, cols(b)], a_ps[b][:], 1.0, None, ALU.mult, ALU.max, accum_out=bmax[:, b : b + 1])
            if b == 0:
                nc.gpsimd.tensor_scalar(nrun[:, 0:1], bmax[:, 0:1], -1.0, 0.0, ALU.mult, ALU.add)
            else:
                eng = nc.vector if b == NB - 1 else nc.gpsimd
                eng.tensor_scalar(nrun[:, b : b + 1], bmax[:, b : b + 1], -1.0, nrun[:, b - 1 : b], ALU.mult, ALU.min)
            if b == NB - 1:
                nc.scalar.copy(ta_sb[:, cols(0)], ta_ps[0][:])
                nc.scalar.activation(fb[:], nrun[:], ACT.Exp, bias=nrun[:, b : b + 1], scale=-1.0)
            nc.scalar.activation(p_sb[:, cols(b)], a_sb[:, cols(b)], ACT.Exp, bias=nrun[:, b : b + 1], accum_out=zb[:, b : b + 1])
        neg_m = nrun[:, NB - 1 : NB]

        px = sb.tile([P, I], F32, name="px")
        ga = sb.tile([P, I], F32, name="ga")
        nc.vector.tensor_copy(ga[:], a_sb[:].indirect(offsets[:]))
        nc.scalar.activation(px[:], ga[:], ACT.Exp, bias=neg_m)
        for b in range(1, NB):
            nc.scalar.copy(ta_sb[:, cols(b)], ta_ps[b][:])

        sumT = [ps.tile([P, BANK], F32, name="sumT%d" % b, tag="x%d" % b) for b in range(NB)]

        def add_turned(b, src, first, last):
            for j in range(BANK // P):
                nc.tensor.matmul(
                    sumT[b][:, j * P : (j + 1) * P],
                    lhsT=src[:, j * P : (j + 1) * P],
                    rhs=ident[:],
                    is_transpose=True,
                    start=first and j == 0,
                    stop=last and j == BANK // P - 1,
                )

        for b in range(NB):
            half, part = divmod(b, 2)
            add_turned(b, base_sb[half][:, cols(part)], True, False)

        nt = sb.tile([P, 1], F32, name="nt")
        t64 = sb.tile([P, G], F32, name="t64")
        nc.scalar.activation(t64[:], tgt[:], ACT.Copy, scale=64.0, accum_out=nt[:])
        xp = sb.tile([P, V], F32, name="xp")
        xps = sb.tile([P, NU * BANK], F32, name="xps")
        acc = sb.tile([P, NB], F32, name="acc")
        acc0 = sb.tile([P, 1], F32, name="acc0")
        z = sb.tile([P, 1], F32, name="z")
        zf = sb.tile([P, NB], F32, name="zf")
        rz = sb.tile([P, 1], F32, name="rz")
        alpha = sb.tile([P, NB], F32, name="alpha")
        nfr = sb.tile([P, NB], F32, name="nfr")

        def product(b, scale):
            nc.vector.scalar_tensor_tensor(xp[:, cols(b)], ta_ps[b][:], scale, p_sb[:, cols(b)], ALU.mult, ALU.mult, accum_out=(acc0[:] if b == 0 else acc[:, b : b + 1]))

        def grouped(t):
            return t[:].rearrange("p (g i) -> p g i", i=GROUP)

        def spread(t):
            return t[:].unsqueeze(2).to_broadcast([P, G, GROUP])

        for b in range(NU):
            product(b, 1.0)
        nc.vector.scalar_tensor_tensor(zf[:], zb[:], -1.0, fb[:], ALU.mult, ALU.mult, accum_out=z[:])
        ssum = sb.tile([P, G], F32, name="ssum")
        nc.vector.tensor_reduce(ssum[:], grouped(px), AX.X, ALU.add)
        nc.vector.reciprocal(rz[:], z[:])
        rs = sb.tile([P, G], F32, name="rs")
        nc.vector.reciprocal(rs[:], ssum[:])
        nc.gpsimd.tensor_scalar(alpha[:], fb[:], rz[:], nt[:], ALU.mult, ALU.mult)
        nc.gpsimd.tensor_scalar(nfr[:], fb[:], rz[:], 0.0, ALU.mult, ALU.add)
        for b in range(NU):
            nc.gpsimd.tensor_scalar(xps[:, cols(b)], xp[:, cols(b)], alpha[:, b : b + 1], 0.0, ALU.mult, ALU.add)
            add_turned(b, xps[:, cols(b)], False, False)
        nc.scalar.activation(acc[:, 0:1], acc0[:], ACT.Copy, scale=alpha[:, 0:1])
        ne64 = sb.tile([P, G], F32, name="ne64")
        nw = sb.tile([P, I], F32, name="nw")
        nc.vector.tensor_tensor(ne64[:], t64[:], rs[:], ALU.mult)
        nc.vector.tensor_tensor(grouped(nw), grouped(px), spread(ne64), ALU.mult)
        for b in range(NU, NB):
            product(b, alpha[:, b : b + 1])
            add_turned(b, xp[:, cols(b)], False, False)
        kk = sb.tile([P, 1], F32, name="kk")
        accf = sb.tile([P, NB], F32, name="accf")
        nc.scalar.activation(accf[:], acc[:], ACT.Copy, accum_out=kk[:])
        beta = sb.tile([P, NB], F32, name="beta")
        nc.scalar.activation(beta[:], nfr[:], ACT.Copy, scale=kk[:])

        y = sb.tile([P, I], F32, name="y")
        ysum = sb.tile([P, G], F32, name="ysum")
        nf = sb.tile([P, G], F32, name="nf")
        v = sb.tile([P, I], F32, name="v")
        halves = [(slice(h * I // 2, (h + 1) * I // 2), slice(h * G // 2, (h + 1) * G // 2), slice(h * 16, (h + 1) * 16)) for h in range(2)]
        for ent, grp, off in halves:
            nc.vector.tensor_tensor(y[:, ent], ta_sb[:].indirect(offsets[:, off]), nw[:, ent], ALU.mult)
        for ent, grp, off in halves:
            nc.vector.tensor_reduce(ysum[:, grp], grouped(y)[:, grp, :], AX.X, ALU.add)
        for ent, grp, off in halves:
            nc.vector.scalar_tensor_tensor(nf[:, grp], ysum[:, grp], -1.0, rs[:, grp], ALU.mult, ALU.mult)
        for ent, grp, off in halves:
            nc.vector.tensor_tensor(grouped(v)[:, grp, :], grouped(px)[:, grp, :], nf[:, grp].unsqueeze(2).to_broadcast([P, G // 2, GROUP]), ALU.mult)
        nc.vector.tensor_tensor(xs2[:].indirect(offsets[:]), y[:], v[:], ALU.add)

        u1 = sb.tile([P, V], F32, name="u1")
        turned = sb.tile([P, V], F32, name="turned")
        dense = [ps.tile([P, BANK], F32, name="dense%d" % b, tag="y%d" % b) for b in range(NB)]

        def scale_p(b):
            nc.scalar.activation(u1[:, cols(b)], p_sb[:, cols(b)], ACT.Copy, scale=beta[:, b : b + 1])
            add_turned(b, u1[:, cols(b)], False, True)

        def turn_back(b):
            nc.scalar.copy(turned[:, cols(b)], sumT[b][:])
            for j in range(BANK // P):
                nc.tensor.transpose(dense[b][:, j * P : (j + 1) * P], turned[:, b * BANK + j * P : b * BANK + (j + 1) * P], ident[:])

        scale_p(0)
        for b in range(1, NB):
            scale_p(b)
            turn_back(b - 1)
        turn_back(NB - 1)

        res = sb.tile([P, V], F32, name="res")
        for lo, hi in ((0, 512), (512, 1024), (1024, 1536), (1536, 2048)):
            b = lo // BANK
            nc.vector.tensor_tensor(res[:, lo:hi], dense[b][:, lo - b * BANK : hi - b * BANK], xs2[:, lo:hi], ALU.add)
            nc.sync.dma_start(out=out[:, lo:hi], in_=res[:, lo:hi])
